import numpy as np
import ml_dtypes


def mxq(x, axis, fmt="e4m3"):
    dtype, down = {"e4m3": (ml_dtypes.float8_e4m3fn, 7), "e5m2": (ml_dtypes.float8_e5m2, 14)}[fmt]
    v = np.moveaxis(np.asarray(x, np.float32).astype(ml_dtypes.bfloat16).astype(np.float64), axis, -1)
    blocks = v.reshape(v.shape[:-1] + (-1, 32))
    amax = np.abs(blocks).max(-1, keepdims=True)
    byte = np.maximum(np.where(amax > 0, np.frexp(amax)[1] - 1 + 127, 0) - down, 1)
    scale = np.exp2(byte - 127.0)
    codes = (blocks / scale).astype(np.float32).astype(dtype).astype(np.float64)
    return np.moveaxis((codes * scale).reshape(v.shape), -1, axis)


WIDE = False


def mx_kscale(k):
    if not WIDE:
        return np.ones(k)
    levels = np.array([10, -10, 5, -5, 0])
    if k % 512:
        return np.exp2(np.random.permutation(np.resize(levels, k // 32))).repeat(32)
    a = np.empty((k // 512, 16))
    for p in range(k // 512):
        a[p, :8] = np.random.permutation(np.resize(levels, 8))
        for g in range(8):
            far = levels[np.abs(levels - a[p, g]) >= 10]
            a[p, g + 8] = far[np.random.randint(len(far))]
    return np.exp2(a.ravel()).repeat(32)


BF16 = ml_dtypes.bfloat16


def bf(x):
    return np.asarray(x, np.float32).astype(BF16)


def f64(x):
    return np.asarray(x).astype(np.float64)

E4M3FN = np.array([(-1.0 if i & 128 else 1.0) * ((1.0 + (i & 7) / 8.0) * 2.0 ** (((i >> 3) & 15) - 7) if i & 120 else (i & 7) * 2.0 ** -9) for i in range(256)])


def e4m3fn_bytes(y):
    return np.clip(np.asarray(y, np.float64), -448.0, 448.0).astype(np.float32).astype(ml_dtypes.float8_e4m3fn).view(np.uint8)


def e4m3fn_values(b):
    return E4M3FN[b]


T, U, K, R, BL = 1024, 1024, 1536, 512, 128
TAU = 32.0
FP8_MAX = 448.0


def setup_inputs():
    s, r = mx_kscale(K), mx_kscale(R)
    a = (K + R) ** -0.25
    e = a * np.random.standard_normal((T, K)) * np.exp(0.3 * np.random.standard_normal((T, 1)))
    o = a * np.random.standard_normal((U, K)) * np.exp(0.3 * np.random.standard_normal((U, 1)))
    p = a * np.random.standard_normal((T, R))
    g = a * np.random.standard_normal((R, U))
    e_norm = np.sqrt((e ** 2).sum(axis=1) + (p ** 2).sum(axis=1))
    o_norm = np.sqrt((o ** 2).sum(axis=1) + (g ** 2).sum(axis=0))
    E, G = e * s, g / r[:, None]
    E_scale = (np.abs(E).reshape(T, K // BL, BL).max(axis=2) / FP8_MAX).astype(np.float32)
    G_scale = (np.abs(G).reshape(R // BL, BL, U // BL, BL).max(axis=(1, 3)) / FP8_MAX).astype(np.float32)
    return {"E_bytes": e4m3fn_bytes(E / np.repeat(f64(E_scale), BL, axis=1)), "E_scale": E_scale,
            "O": bf(o / s), "P": bf(p * r),
            "G_bytes": e4m3fn_bytes(G / np.repeat(np.repeat(f64(G_scale), BL, axis=0), BL, axis=1)), "G_scale": G_scale,
            "e_norm": bf(e_norm), "o_norm": bf(o_norm)}


def reference(E_bytes, E_scale, O, P, G_bytes, G_scale, e_norm, o_norm):
    E = e4m3fn_values(E_bytes) * np.repeat(f64(E_scale), BL, axis=1)
    G = e4m3fn_values(G_bytes) * np.repeat(np.repeat(f64(G_scale), BL, axis=0), BL, axis=1)
    content = mxq(E, 1, "e4m3") @ mxq(f64(O), 1, "e4m3").T
    position = mxq(f64(P), 1, "e4m3") @ mxq(G, 0, "e4m3")
    joint = content + position
    return joint / f64(e_norm)[:, None] / f64(o_norm)[None, :] * TAU

@@ -1,0 +1,270 @@
+from contextlib import ExitStack
+
+import concourse.mybir as mybir
+from concourse.masks import make_identity
+
+T, U, K, R = 1024, 1024, 1536, 512
+FLOPS = 2 * T * U * (K + R)
+
+F32 = mybir.dt.float32
+BF16 = mybir.dt.bfloat16
+U32 = mybir.dt.uint32
+U8 = mybir.dt.uint8
+F8 = mybir.dt.float8_e4m3fn
+FP8X4 = mybir.dt.float8_e4m3fn_x4
+MULT = mybir.AluOpType.mult
+COPY = mybir.ActivationFunctionType.Copy
+
+NP = 128
+PASS = 512
+EP = K // PASS
+PAIR = 256
+NPAIR = T // PAIR
+
+
+def tile_token_merging_cosine_scores_d9_kernel(
+    tc, E_bytes, E_scale, O, P, G_bytes, G_scale, e_norm, o_norm, out
+):
+    nc = tc.nc
+    with ExitStack() as ctx:
+        keep = ctx.enter_context(tc.tile_pool(name="keep", bufs=1))
+        stage = ctx.enter_context(tc.tile_pool(name="stage", bufs=8))
+        results = ctx.enter_context(tc.tile_pool(name="results", bufs=8))
+        turn = ctx.enter_context(tc.psum_pool(name="turn", bufs=4))
+        accs = ctx.enter_context(tc.psum_pool(name="accs", bufs=4))
+        ctx.enter_context(tc.manual_schedule())
+
+        e_rows = E_bytes.rearrange("(p m) k -> p m k", m=8)
+        p_rows = P.rearrange("(p m) k -> p m k", m=8)
+        out_rows = out.rearrange("(p m) n -> p m n", m=8)
+        g_rows = G_bytes.rearrange("(p t) n -> p t n", t=4)
+
+        es = keep.tile([NP, 8, 12], F32, name="es")
+        nc.scalar.dma_start(out=es[:], in_=E_scale.rearrange("(p m) b -> p m b", m=8))
+        en = keep.tile([NP, 8], BF16, name="en")
+        on = keep.tile([NP, 8], BF16, name="on")
+        gs = keep.tile([NP, 8], F32, name="gs")
+
+        o_sb, e8, p_sb, g8 = [], [], [], []
+        for j in range(NPAIR):
+            o_t = keep.tile([NP, 2, K], BF16, name=f"o_sb{j}", align_bytes=64)
+            o_sb.append(o_t)
+            e_t = keep.tile([NP, 2, K], U8, name=f"e8_{j}", align_bytes=64)
+            e8.append(e_t)
+            p_t = keep.tile([NP, 2, R], BF16, name=f"p_sb{j}", align_bytes=64)
+            p_sb.append(p_t)
+        for h in range(2):
+            g_t = keep.tile([NP, 4, 512], U8, name=f"g8_{h}", align_bytes=64)
+            g8.append(g_t)
+
+        def load_o(j, cols):
+            nc.sync.dma_start(
+                out=o_sb[j][:, :, cols],
+                in_=O[PAIR * j : PAIR * (j + 1), cols].rearrange("(t p) k -> p t k", p=NP),
+            )
+
+        def load_e(i):
+            nc.sync.dma_start(out=e8[i][:], in_=e_rows[:, 2 * i : 2 * i + 2, :])
+
+        def load_p(i):
+            nc.sync.dma_start(out=p_sb[i][:], in_=p_rows[:, 2 * i : 2 * i + 2, :])
+
+        def load_g(h):
+            nc.sync.dma_start(out=g8[h][:], in_=g_rows[:, :, 512 * h : 512 * h + 512])
+
+        load_o(0, slice(0, PASS))
+        load_e(0)
+        load_o(0, slice(PASS, 2 * PASS))
+        load_o(0, slice(2 * PASS, K))
+        load_p(0)
+        load_g(0)
+        nc.scalar.dma_start(out=on[:], in_=o_norm.rearrange("(p m) -> p m", m=8))
+        nc.scalar.dma_start(out=en[:], in_=e_norm.rearrange("(p m) -> p m", m=8))
+        for a in range(4):
+            nc.scalar.dma_start(out=gs[32 * a : 32 * a + 32, :], in_=G_scale[a].partition_broadcast(32))
+        for j in range(1, NPAIR):
+            load_o(j, slice(0, K))
+            load_e(j)
+            load_p(j)
+            if j == 2:
+                load_g(1)
+
+        ident = keep.tile([NP, NP], F32, name="ident")
+        make_identity(nc, ident[:])
+
+        ew = [[None] * EP for i in range(NPAIR)]
+        for i in range(NPAIR):
+            for g in range(EP):
+                w_t = keep.tile([NP, 2, PASS], BF16, name=f"ew{i}_{g}", align_bytes=64)
+                ew[i][g] = w_t
+        gw = []
+        for h in range(2):
+            w_t = keep.tile([NP, 4, 512], BF16, name=f"gw{h}", align_bytes=64)
+            gw.append(w_t)
+
+        codes, scales = {}, {}
+
+        def scale_list(i):
+            return [(i, g, mt, b) for g in range(EP) for mt in range(2) for b in range(4)]
+
+        def scale_e(i, g, mt, b):
+            src = e8[i][:, mt, PASS * g + 128 * b : PASS * g + 128 * b + 128].bitcast(F8)
+            dst = ew[i][g][:, mt, :].rearrange("q (u p e) -> q p u e", u=2, e=2)[:, 32 * b : 32 * b + 32]
+            nc.vector.tensor_scalar(
+                out=dst,
+                in0=src.rearrange("q (p u e) -> q p u e", u=2, e=2),
+                scalar1=es[:, 2 * i + mt, 4 * g + b : 4 * g + b + 1],
+                scalar2=None,
+                op0=MULT,
+            )
+
+        def turned(source, key):
+            bank = turn.tile([NP, 2, 2, NP], F32, name="bank")
+            for t in range(2):
+                for u in range(2):
+                    nc.tensor.transpose(bank[:, t, u, :], source(t, u), ident[:])
+            grouped = stage.tile([NP, 4 * PAIR], BF16, name="grouped", align_bytes=64)
+            nc.scalar.copy(
+                out=grouped[:].bitcast(F32).rearrange("p (t r u) -> p t r u", t=2, u=2),
+                in_=bank[:].rearrange("p t u r -> p t r u"),
+            )
+            return (grouped, key)
+
+        def quantize(item):
+            grouped, key = item
+            c_t = keep.tile([NP, PAIR], U32, name="codes_%s_%d_%d" % key, align_bytes=64)
+            s_t = keep.tile([NP, PAIR], U8, name="scales_%s_%d_%d" % key, align_bytes=64)
+            nc.vector.quantize_mx(out=c_t[:].bitcast(FP8X4), scales=s_t[:], in_=grouped[:])
+            codes[key], scales[key] = c_t, s_t
+
+        def turn_o(j):
+            def words(g):
+                return lambda t, u: o_sb[j][:, t, PASS * g : PASS * (g + 1)].bitcast(F32)[:, u:PAIR:2]
+
+            return [turned(words(g), ("O", j, g)) for g in range(EP)]
+
+        def turn_e(i):
+            def words(g):
+                return lambda t, u: ew[i][g][:, t, PAIR * u : PAIR * (u + 1)].bitcast(F32)
+
+            def p_words(t, u):
+                return p_sb[i][:, t, :].bitcast(F32)[:, u:PAIR:2]
+
+            done = [turned(p_words, ("E", i, EP))]
+            done.extend([turned(words(g), ("E", i, g)) for g in range(EP)])
+            return done
+
+        def widen_g(h, on_vector):
+            src = g8[h][:].rearrange("p t n -> p (t n)").bitcast(F8)
+            dst = gw[h][:].rearrange("p t n -> p (t n)")
+            if on_vector:
+                nc.vector.tensor_copy(out=dst, in_=src)
+            else:
+                nc.scalar.copy(out=dst, in_=src)
+
+        def group_g(j, on_vector):
+            grouped = stage.tile([NP, 4 * PAIR], BF16, name="grouped", align_bytes=64)
+            dst = grouped[:].rearrange("p (c t) -> p c t", t=4)
+            src = gw[j // 2][:].rearrange("p t n -> p n t")
+            for b in range(2):
+                c0 = PAIR * (j % 2) + 128 * b
+                col = gs[:, 2 * j + b : 2 * j + b + 1]
+                if on_vector:
+                    nc.vector.tensor_scalar(
+                        out=dst[:, 128 * b : 128 * b + 128, :], in0=src[:, c0 : c0 + 128, :],
+                        scalar1=col, scalar2=None, op0=MULT,
+                    )
+                else:
+                    nc.scalar.activation(
+                        out=dst[:, 128 * b : 128 * b + 128, :], in_=src[:, c0 : c0 + 128, :],
+                        func=COPY, scale=col,
+                    )
+            return (grouped, ("O", j, EP))
+
+        re32 = keep.tile([NP, 8], F32, name="re32")
+        re = keep.tile([NP, 8], F32, name="re")
+        r8 = keep.tile([NP, 8], F32, name="r8")
+        ro = keep.tile([NP, NP, 8], F32, name="ro")
+
+        def norms():
+            nc.vector.reciprocal(out=r8[:], in_=on[:])
+            nc.vector.reciprocal(out=re[:], in_=en[:])
+            nc.vector.tensor_scalar(out=re32[:], in0=re[:], scalar1=32.0, scalar2=None, op0=MULT)
+
+        def spread_o_norm():
+            for h in range(2):
+                bank = turn.tile([NP, 4, NP], F32, name="bank")
+                for q in range(4):
+                    m = 4 * h + q
+                    nc.tensor.transpose(bank[:, q, :], r8[:, m : m + 1].to_broadcast([NP, NP]), ident[:])
+                nc.vector.tensor_copy(out=ro[:, :, 4 * h : 4 * h + 4], in_=bank[:].rearrange("p q n -> p n q"))
+
+        ro_row = ro[:].rearrange("p n m -> p (n m)")
+
+        def multiply(i, j):
+            acc = accs.tile([NP, 2, PAIR], F32, name="acc")
+            for mt in range(2):
+                for g in range(EP + 1):
+                    cols = slice(128 * mt, 128 * mt + 128)
+                    nc.tensor.matmul_mx(
+                        out=acc[:, mt, :],
+                        lhsT=codes["E", i, g][:, cols].bitcast(FP8X4),
+                        lhsT_scale=scales["E", i, g][:, cols],
+                        rhs=codes["O", j, g][:].bitcast(FP8X4),
+                        rhs_scale=scales["O", j, g][:],
+                        start=(g == 0),
+                        stop=(g == EP),
+                    )
+            return (acc, i, j)
+
+        def finish(item):
+            acc, i, j = item
+            res = results.tile([NP, 2, PAIR], F32, name="res")
+            for mt in range(2):
+                m = 2 * i + mt
+                nc.vector.scalar_tensor_tensor(
+                    out=res[:, mt, :], in0=acc[:, mt, :], scalar=re32[:, m : m + 1],
+                    in1=ro_row[:, PAIR * j : PAIR * (j + 1)], op0=MULT, op1=MULT,
+                )
+            nc.sync.dma_start(out=out_rows[:, 2 * i : 2 * i + 2, PAIR * j : PAIR * (j + 1)], in_=res[:])
+
+        for args in scale_list(0):
+            scale_e(*args)
+        norms()
+        todo = []
+        enabled = []
+        for n in range(2 * NPAIR):
+            s = n // 2
+            if n % 2 == 0:
+                items = turn_o(s)
+                fresh = [(i, s) for i in range(s)]
+                if s == 1:
+                    items.append(group_g(1, False))
+                elif s == 2:
+                    widen_g(1, False)
+                    items.append(group_g(2, False))
+                elif s == 3:
+                    items.append(group_g(3, False))
+            else:
+                items = turn_e(s)
+                fresh = [(s, j) for j in range(s + 1)]
+                if s == 0:
+                    spread_o_norm()
+                    widen_g(0, True)
+                    items.append(group_g(0, True))
+                if s + 1 < NPAIR:
+                    todo.extend(scale_list(s + 1))
+            accs_now = [multiply(i, j) for (i, j) in enabled]
+            share = len(todo) if n % 2 == 0 else len(todo) // 2
+            per = -(-share // len(items)) if items else 0
+            taken = 0
+            for item in items:
+                for x in range(min(per, share - taken)):
+                    scale_e(*todo.pop(0))
+                    taken += 1
+                quantize(item)
+            for item in accs_now:
+                finish(item)
+            enabled = fresh
+        for (i, j) in enabled:
+            finish(multiply(i, j))

@@ -20,6 +20,7 @@ PASS = 512
 EP = K // PASS
 PAIR = 256
 NPAIR = T // PAIR
+CFG = {'dummy': [0, 2, 2, 0, 0, 0, 0, 2, 0, 2, 0, 0], 'sc': [0, 0, 0, 4, 4, 4, 12, 14, 17, 18, 23, 24], 'norm': 1, 'ql': 1, 'cv': [3, 19, 17], 'ro': 8, 'rov': False, 'g': [0, 6, 16, 22], 'gw': [True, False, True, True], 'gg': [True, True, False, False], 'gl': 1, 'efirst': False, 'pp': {24: False, 14: True, 22: False, 16: True, 3: False, 23: False, 17: False, 21: False, 1: False, 15: False}, 'se': [], 'pa': 4, 'b': [10, 13, 17, 17, 20, 20, 23, 24, 24, 28, 29, 29, 30, 30, 33, 34]}
 
 
 def tile_token_merging_cosine_scores_d9_kernel(
@@ -53,8 +54,8 @@ def tile_token_merging_cosine_scores_d9_kernel(
             e8.append(e_t)
             p_t = keep.tile([NP, 2, R], BF16, name=f"p_sb{j}", align_bytes=64)
             p_sb.append(p_t)
-        for h in range(2):
-            g_t = keep.tile([NP, 4, 512], U8, name=f"g8_{h}", align_bytes=64)
+        for h in range(NPAIR):
+            g_t = keep.tile([NP, 4, PAIR], U8, name=f"g8_{h}", align_bytes=64)
             g8.append(g_t)
 
         def load_o(j, cols):
@@ -63,21 +64,28 @@ def tile_token_merging_cosine_scores_d9_kernel(
                 in_=O[PAIR * j : PAIR * (j + 1), cols].rearrange("(t p) k -> p t k", p=NP),
             )
 
-        def load_e(i):
-            nc.sync.dma_start(out=e8[i][:], in_=e_rows[:, 2 * i : 2 * i + 2, :])
+        def load_e(i, cols=slice(0, K)):
+            nc.sync.dma_start(out=e8[i][:, :, cols], in_=e_rows[:, 2 * i : 2 * i + 2, cols])
 
         def load_p(i):
             nc.sync.dma_start(out=p_sb[i][:], in_=p_rows[:, 2 * i : 2 * i + 2, :])
 
         def load_g(h):
-            nc.sync.dma_start(out=g8[h][:], in_=g_rows[:, :, 512 * h : 512 * h + 512])
+            nc.sync.dma_start(out=g8[h][:], in_=g_rows[:, :, PAIR * h : PAIR * (h + 1)])
 
-        load_o(0, slice(0, PASS))
-        load_e(0)
+        first, second = slice(0, PASS), slice(PASS, K)
+        if CFG["efirst"]:
+            load_e(0, first)
+            load_o(0, first)
+            load_e(0, second)
+        else:
+            load_o(0, first)
+            load_e(0, first)
+            load_e(0, second)
         load_o(0, slice(PASS, 2 * PASS))
-        load_o(0, slice(2 * PASS, K))
-        load_p(0)
         load_g(0)
+        load_p(0)
+        load_o(0, slice(2 * PASS, K))
         nc.scalar.dma_start(out=on[:], in_=o_norm.rearrange("(p m) -> p m", m=8))
         nc.scalar.dma_start(out=en[:], in_=e_norm.rearrange("(p m) -> p m", m=8))
         for a in range(4):
@@ -86,8 +94,7 @@ def tile_token_merging_cosine_scores_d9_kernel(
             load_o(j, slice(0, K))
             load_e(j)
             load_p(j)
-            if j == 2:
-                load_g(1)
+            load_g(j)
 
         ident = keep.tile([NP, NP], F32, name="ident")
         make_identity(nc, ident[:])
@@ -98,8 +105,8 @@ def tile_token_merging_cosine_scores_d9_kernel(
                 w_t = keep.tile([NP, 2, PASS], BF16, name=f"ew{i}_{g}", align_bytes=64)
                 ew[i][g] = w_t
         gw = []
-        for h in range(2):
-            w_t = keep.tile([NP, 4, 512], BF16, name=f"gw{h}", align_bytes=64)
+        for h in range(NPAIR):
+            w_t = keep.tile([NP, 4, PAIR], BF16, name=f"gw{h}", align_bytes=64)
             gw.append(w_t)
 
         codes, scales = {}, {}
@@ -118,13 +125,14 @@ def tile_token_merging_cosine_scores_d9_kernel(
                 op0=MULT,
             )
 
-        def turned(source, key):
+        def turned(source, key, on_vector):
             bank = turn.tile([NP, 2, 2, NP], F32, name="bank")
             for t in range(2):
                 for u in range(2):
                     nc.tensor.transpose(bank[:, t, u, :], source(t, u), ident[:])
             grouped = stage.tile([NP, 4 * PAIR], BF16, name="grouped", align_bytes=64)
-            nc.scalar.copy(
+            copy = nc.vector.tensor_copy if on_vector else nc.scalar.copy
+            copy(
                 out=grouped[:].bitcast(F32).rearrange("p (t r u) -> p t r u", t=2, u=2),
                 in_=bank[:].rearrange("p t u r -> p t r u"),
             )
@@ -137,22 +145,34 @@ def tile_token_merging_cosine_scores_d9_kernel(
             nc.vector.quantize_mx(out=c_t[:].bitcast(FP8X4), scales=s_t[:], in_=grouped[:])
             codes[key], scales[key] = c_t, s_t
 
-        def turn_o(j):
-            def words(g):
-                return lambda t, u: o_sb[j][:, t, PASS * g : PASS * (g + 1)].bitcast(F32)[:, u:PAIR:2]
+        perm = {}
 
-            return [turned(words(g), ("O", j, g)) for g in range(EP)]
+        def permute(unit, on_vector):
+            kind, i, g = unit
+            o_t = keep.tile([NP, 2, PASS], BF16, name="perm_%s_%d_%d" % unit, align_bytes=64)
+            src = o_sb[i][:, :, PASS * g : PASS * (g + 1)] if kind == "O" else p_sb[i][:]
+            copy = nc.vector.tensor_copy if on_vector else nc.scalar.copy
+            copy(
+                out=o_t[:].bitcast(F32).rearrange("p t (u w) -> p t u w", u=2),
+                in_=src.bitcast(F32).rearrange("p t (w u) -> p t u w", u=2),
+            )
+            perm[unit] = o_t
 
-        def turn_e(i):
-            def words(g):
-                return lambda t, u: ew[i][g][:, t, PAIR * u : PAIR * (u + 1)].bitcast(F32)
+        def turn_bank(unit, on_vector):
+            kind, i, g = unit
 
-            def p_words(t, u):
-                return p_sb[i][:, t, :].bitcast(F32)[:, u:PAIR:2]
+            def words(t, u):
+                if unit in perm:
+                    return perm[unit][:, t, PAIR * u : PAIR * (u + 1)].bitcast(F32)
+                if kind == "O":
+                    return o_sb[i][:, t, PASS * g : PASS * (g + 1)].bitcast(F32)[:, u:PAIR:2]
+                if g == EP:
+                    return p_sb[i][:, t, :].bitcast(F32)[:, u:PAIR:2]
+                if 3 * i + g in CFG["se"]:
+                    return ew[i][g][:, t, :].bitcast(F32)[:, u:PAIR:2]
+                return ew[i][g][:, t, PAIR * u : PAIR * (u + 1)].bitcast(F32)
 
-            done = [turned(p_words, ("E", i, EP))]
-            done.extend([turned(words(g), ("E", i, g)) for g in range(EP)])
-            return done
+            return turned(words, unit, on_vector)
 
         def widen_g(h, on_vector):
             src = g8[h][:].rearrange("p t n -> p (t n)").bitcast(F8)
@@ -165,9 +185,9 @@ def tile_token_merging_cosine_scores_d9_kernel(
         def group_g(j, on_vector):
             grouped = stage.tile([NP, 4 * PAIR], BF16, name="grouped", align_bytes=64)
             dst = grouped[:].rearrange("p (c t) -> p c t", t=4)
-            src = gw[j // 2][:].rearrange("p t n -> p n t")
+            src = gw[j][:].rearrange("p t n -> p n t")
             for b in range(2):
-                c0 = PAIR * (j % 2) + 128 * b
+                c0 = 128 * b
                 col = gs[:, 2 * j + b : 2 * j + b + 1]
                 if on_vector:
                     nc.vector.tensor_scalar(
@@ -191,13 +211,14 @@ def tile_token_merging_cosine_scores_d9_kernel(
             nc.vector.reciprocal(out=re[:], in_=en[:])
             nc.vector.tensor_scalar(out=re32[:], in0=re[:], scalar1=32.0, scalar2=None, op0=MULT)
 
-        def spread_o_norm():
+        def spread_o_norm(on_vector):
             for h in range(2):
                 bank = turn.tile([NP, 4, NP], F32, name="bank")
                 for q in range(4):
                     m = 4 * h + q
                     nc.tensor.transpose(bank[:, q, :], r8[:, m : m + 1].to_broadcast([NP, NP]), ident[:])
-                nc.vector.tensor_copy(out=ro[:, :, 4 * h : 4 * h + 4], in_=bank[:].rearrange("p q n -> p n q"))
+                copy = nc.vector.tensor_copy if on_vector else nc.scalar.copy
+                copy(out=ro[:, :, 4 * h : 4 * h + 4], in_=bank[:].rearrange("p q n -> p n q"))
 
         ro_row = ro[:].rearrange("p n m -> p (n m)")
 
@@ -226,45 +247,80 @@ def tile_token_merging_cosine_scores_d9_kernel(
                     out=res[:, mt, :], in0=acc[:, mt, :], scalar=re32[:, m : m + 1],
                     in1=ro_row[:, PAIR * j : PAIR * (j + 1)], op0=MULT, op1=MULT,
                 )
-            nc.sync.dma_start(out=out_rows[:, 2 * i : 2 * i + 2, PAIR * j : PAIR * (j + 1)], in_=res[:])
+                if (i, j) == (NPAIR - 1, NPAIR - 1):
+                    nc.sync.dma_start(out=out_rows[:, m, PAIR * j : PAIR * (j + 1)], in_=res[:, mt, :])
+            if (i, j) != (NPAIR - 1, NPAIR - 1):
+                nc.sync.dma_start(out=out_rows[:, 2 * i : 2 * i + 2, PAIR * j : PAIR * (j + 1)], in_=res[:])
 
-        for args in scale_list(0):
-            scale_e(*args)
-        norms()
-        todo = []
-        enabled = []
-        for n in range(2 * NPAIR):
-            s = n // 2
-            if n % 2 == 0:
-                items = turn_o(s)
-                fresh = [(i, s) for i in range(s)]
-                if s == 1:
-                    items.append(group_g(1, False))
-                elif s == 2:
-                    widen_g(1, False)
-                    items.append(group_g(2, False))
-                elif s == 3:
-                    items.append(group_g(3, False))
-            else:
-                items = turn_e(s)
-                fresh = [(s, j) for j in range(s + 1)]
-                if s == 0:
-                    spread_o_norm()
-                    widen_g(0, True)
-                    items.append(group_g(0, True))
-                if s + 1 < NPAIR:
-                    todo.extend(scale_list(s + 1))
-            accs_now = [multiply(i, j) for (i, j) in enabled]
-            share = len(todo) if n % 2 == 0 else len(todo) // 2
-            per = -(-share // len(items)) if items else 0
-            taken = 0
-            for item in items:
-                for x in range(min(per, share - taken)):
-                    scale_e(*todo.pop(0))
-                    taken += 1
-                quantize(item)
-            for item in accs_now:
-                finish(item)
-            enabled = fresh
-        for (i, j) in enabled:
-            finish(multiply(i, j))
+        warm = keep.tile([NP, 512], BF16, name="warm")
+        if any(CFG["dummy"]):
+            nc.gpsimd.memset(warm[:], 1.0)
+
+        def dummy(n):
+            if n:
+                acc = accs.tile([NP, 2, PAIR], F32, name="acc")
+                for x in range(n):
+                    nc.tensor.matmul(acc[:].rearrange("p a n -> p (a n)"), lhsT=warm[:, :NP], rhs=warm[:], start=True, stop=True)
+
+        units = []
+        for s in range(NPAIR):
+            units.extend([("O", s, g) for g in range(EP)])
+            units.extend([("E", s, g) for g in (EP, 0, 1, 2)])
+        chunks = [("E", i, g) for i in range(NPAIR) for g in range(EP)]
+        blocks = []
+        for s in range(NPAIR):
+            blocks.extend([(i, s) for i in range(s)])
+            blocks.extend([(s, j) for j in range(s + 1)])
+
+        def scale_chunk(unit):
+            kind, i, g = unit
+            for mt in range(2):
+                for b in range(4):
+                    if 3 * i + g in CFG["se"]:
+                        src = e8[i][:, mt, PASS * g + 128 * b : PASS * g + 128 * b + 128].bitcast(F8)
+                        nc.scalar.activation(out=ew[i][g][:, mt, 128 * b : 128 * b + 128], in_=src, func=COPY,
+                                             scale=es[:, 2 * i + mt, 4 * g + b : 4 * g + b + 1])
+                    else:
+                        scale_e(i, g, mt, b)
+
+        dummy(CFG["dummy"][0])
+        waiting, made = [], []
+        bi = ci = gi = 0
+        for x in range(len(units) + 8):
+            while ci < len(chunks) and CFG["sc"][ci] <= x:
+                scale_chunk(chunks[ci])
+                ci += 1
+            for y in range(x + 1 if x == 0 else x + CFG["pa"], x + CFG["pa"] + 1):
+                if y < len(units) and y in CFG["pp"] and units[y] not in perm:
+                    permute(units[y], CFG["pp"][y])
+            if x == CFG["norm"]:
+                norms()
+            if x < len(units):
+                waiting.append((x + CFG["ql"], turn_bank(units[x], x in CFG["cv"])))
+            if x + 1 < len(CFG["dummy"]):
+                dummy(CFG["dummy"][x + 1])
+            if x == CFG["ro"]:
+                spread_o_norm(CFG["rov"])
+            while gi < NPAIR and CFG["g"][gi] <= x:
+                widen_g(gi, CFG["gw"][gi])
+                waiting.append((x + CFG["gl"], group_g(gi, CFG["gg"][gi])))
+                gi += 1
+            for entry in [e for e in waiting if e[0] <= x]:
+                quantize(entry[1])
+                waiting.remove(entry)
+            for d in made:
+                finish(d)
+            made = []
+            while bi < len(blocks) and CFG["b"][bi] <= x:
+                i, j = blocks[bi]
+                for entry in list(waiting):
+                    key = entry[1][1]
+                    if key[:2] == ("E", i) or key[:2] == ("O", j):
+                        quantize(entry[1])
+                        waiting.remove(entry)
+                if len(made) == 3:
+                    finish(made.pop(0))
+                made.append(multiply(i, j))
+                bi += 1
+        for d in made:
+            finish(d)

@@ -20,7 +20,7 @@ PASS = 512
 EP = K // PASS
 PAIR = 256
 NPAIR = T // PAIR
-CFG = {'dummy': [0, 2, 2, 0, 0, 0, 0, 2, 0, 2, 0, 0], 'sc': [0, 0, 0, 4, 4, 4, 12, 14, 17, 18, 23, 24], 'norm': 1, 'ql': 1, 'cv': [3, 19, 17], 'ro': 8, 'rov': False, 'g': [0, 6, 16, 22], 'gw': [True, False, True, True], 'gg': [True, True, False, False], 'gl': 1, 'efirst': False, 'pp': {24: False, 14: True, 22: False, 16: True, 3: False, 23: False, 17: False, 21: False, 1: False, 15: False}, 'se': [], 'pa': 4, 'b': [10, 13, 17, 17, 20, 20, 23, 24, 24, 28, 29, 29, 30, 30, 33, 34]}
+CFG = {'dummy': [0, 2, 0, 2, 0, 2, 0, 0, 0, 0, 0, 0, 0, 0], 'norm': 1, 'ql': 2, 'cv': [], 'ro': 7, 'rov': False, 'order': [('O', 0), ('E', 0), ('E', 1), ('O', 1), ('E', 2), ('E', 3), ('O', 2), ('E', 4), ('E', 5), ('O', 3), ('E', 6), ('E', 7)], 'sd': [13, 3, 3, 3, 3, 3, 3, 3], 'gd': [-1, -3, -3, -3], 'gw': [True, True, True, True], 'gg': [True, True, False, False], 'gl': 2, 'split': [(0, 0), (1, 0), (2, 0), (0, 1), (1, 1), (2, 1), (3, 1), (4, 1), (5, 1)], 'bd': {}, 'lag': 4, 'se': [(0, 1), (1, 1), (2, 1), (3, 1), (4, 1), (5, 1), (6, 1), (7, 1)], 'vc': [], 'pp': {15: False, 16: False, 22: False, 23: False, 24: False, 26: False}, 'pa': 4, 'head': ['o0', 'e0', 'o1', 'o2', 'g', 'p', 'e1'], 'ord': 'b', 'sd1': 4, 'gd0': 0, 'gwv': 0, 'ggv': 4, 'sp0': 1, 'sp1': 2, 'sem': 4, 'seg': (0,), 'po': 3, 'pog': (1,), 'pm': 8, 'pv': False, 'cvs': 28, 'cvn': 9, 'cve': 14, 'd0': 3, 'd1': 8, 'dn': 2, 'dc': 2}
 
 
 def tile_token_merging_cosine_scores_d9_kernel(
@@ -73,37 +73,38 @@ def tile_token_merging_cosine_scores_d9_kernel(
         def load_g(h):
             nc.sync.dma_start(out=g8[h][:], in_=g_rows[:, :, PAIR * h : PAIR * (h + 1)])
 
-        first, second = slice(0, PASS), slice(PASS, K)
-        if CFG["efirst"]:
-            load_e(0, first)
-            load_o(0, first)
-            load_e(0, second)
-        else:
-            load_o(0, first)
-            load_e(0, first)
-            load_e(0, second)
-        load_o(0, slice(PASS, 2 * PASS))
-        load_g(0)
-        load_p(0)
-        load_o(0, slice(2 * PASS, K))
+        def load_e_tile(m, cols=slice(0, K)):
+            nc.sync.dma_start(out=e8[m // 2][:, m % 2, cols], in_=e_rows[:, m, cols])
+
+        for what in CFG["head"]:
+            if what[0] == "o":
+                load_o(0, slice(PASS * int(what[1]), PASS * int(what[1]) + PASS))
+            elif what[0] == "e":
+                load_e_tile(int(what[1]))
+            elif what[0] == "p":
+                load_p(0)
+            else:
+                load_g(0)
         nc.scalar.dma_start(out=on[:], in_=o_norm.rearrange("(p m) -> p m", m=8))
         nc.scalar.dma_start(out=en[:], in_=e_norm.rearrange("(p m) -> p m", m=8))
         for a in range(4):
             nc.scalar.dma_start(out=gs[32 * a : 32 * a + 32, :], in_=G_scale[a].partition_broadcast(32))
-        for j in range(1, NPAIR):
-            load_o(j, slice(0, K))
-            load_e(j)
-            load_p(j)
-            load_g(j)
+        for kind, j in CFG["order"]:
+            if kind == "O" and j > 0:
+                load_o(j, slice(0, K))
+                load_g(j)
+            elif kind == "E" and j % 2 == 0 and j > 0:
+                load_e(j // 2)
+                load_p(j // 2)
 
         ident = keep.tile([NP, NP], F32, name="ident")
         make_identity(nc, ident[:])
 
-        ew = [[None] * EP for i in range(NPAIR)]
-        for i in range(NPAIR):
+        ew = {}
+        for m in range(8):
             for g in range(EP):
-                w_t = keep.tile([NP, 2, PASS], BF16, name=f"ew{i}_{g}", align_bytes=64)
-                ew[i][g] = w_t
+                w_t = keep.tile([NP, PASS], BF16, name=f"ew{m}_{g}", align_bytes=64)
+                ew[m, g] = w_t
         gw = []
         for h in range(NPAIR):
             w_t = keep.tile([NP, 4, PAIR], BF16, name=f"gw{h}", align_bytes=64)
@@ -111,19 +112,19 @@ def tile_token_merging_cosine_scores_d9_kernel(
 
         codes, scales = {}, {}
 
-        def scale_list(i):
-            return [(i, g, mt, b) for g in range(EP) for mt in range(2) for b in range(4)]
-
-        def scale_e(i, g, mt, b):
-            src = e8[i][:, mt, PASS * g + 128 * b : PASS * g + 128 * b + 128].bitcast(F8)
-            dst = ew[i][g][:, mt, :].rearrange("q (u p e) -> q p u e", u=2, e=2)[:, 32 * b : 32 * b + 32]
-            nc.vector.tensor_scalar(
-                out=dst,
-                in0=src.rearrange("q (p u e) -> q p u e", u=2, e=2),
-                scalar1=es[:, 2 * i + mt, 4 * g + b : 4 * g + b + 1],
-                scalar2=None,
-                op0=MULT,
-            )
+        def scale_e(m, g):
+            for b in range(4):
+                c0 = PASS * g + 128 * b
+                src = e8[m // 2][:, m % 2, c0 : c0 + 128].bitcast(F8)
+                col = es[:, m, 4 * g + b : 4 * g + b + 1]
+                if (m, g) in CFG["se"]:
+                    nc.scalar.activation(out=ew[m, g][:, 128 * b : 128 * b + 128], in_=src, func=COPY, scale=col)
+                elif (m, g) in CFG["vc"]:
+                    nc.vector.tensor_scalar(out=ew[m, g][:, 128 * b : 128 * b + 128], in0=src, scalar1=col, scalar2=None, op0=MULT)
+                else:
+                    dst = ew[m, g][:].rearrange("q (u p e) -> q p u e", u=2, e=2)[:, 32 * b : 32 * b + 32]
+                    nc.vector.tensor_scalar(out=dst, in0=src.rearrange("q (p u e) -> q p u e", u=2, e=2),
+                                            scalar1=col, scalar2=None, op0=MULT)
 
         def turned(source, key, on_vector):
             bank = turn.tile([NP, 2, 2, NP], F32, name="bank")
@@ -140,17 +141,34 @@ def tile_token_merging_cosine_scores_d9_kernel(
 
         def quantize(item):
             grouped, key = item
-            c_t = keep.tile([NP, PAIR], U32, name="codes_%s_%d_%d" % key, align_bytes=64)
-            s_t = keep.tile([NP, PAIR], U8, name="scales_%s_%d_%d" % key, align_bytes=64)
-            nc.vector.quantize_mx(out=c_t[:].bitcast(FP8X4), scales=s_t[:], in_=grouped[:])
-            codes[key], scales[key] = c_t, s_t
+            kind, i, g = key
+            if kind == "O":
+                home, at = ("O", i // 2, g), PAIR * (i % 2)
+                if home not in codes:
+                    c_t = keep.tile([NP, 2 * PAIR], U32, name="codes_%s_%d_%d" % home, align_bytes=64)
+                    s_t = keep.tile([NP, 2 * PAIR], U8, name="scales_%s_%d_%d" % home, align_bytes=64)
+                    codes[home], scales[home] = c_t, s_t
+            else:
+                home, at = key, 0
+                c_t = keep.tile([NP, PAIR], U32, name="codes_%s_%d_%d" % home, align_bytes=64)
+                s_t = keep.tile([NP, PAIR], U8, name="scales_%s_%d_%d" % home, align_bytes=64)
+                codes[home], scales[home] = c_t, s_t
+            nc.vector.quantize_mx(
+                out=codes[home][:, at : at + PAIR].bitcast(FP8X4),
+                scales=scales[home][:, at : at + PAIR],
+                in_=grouped[:],
+            )
 
         perm = {}
+        FIRST = {0: (EP, 0), 1: (1, 2)}
 
         def permute(unit, on_vector):
             kind, i, g = unit
-            o_t = keep.tile([NP, 2, PASS], BF16, name="perm_%s_%d_%d" % unit, align_bytes=64)
-            src = o_sb[i][:, :, PASS * g : PASS * (g + 1)] if kind == "O" else p_sb[i][:]
+            if kind == "O":
+                src, n = o_sb[i][:, :, PASS * g : PASS * (g + 1)], 2
+            else:
+                src, n = p_sb[i // 2][:, i % 2 : i % 2 + 1, :], 1
+            o_t = keep.tile([NP, n, PASS], BF16, name="perm_%s_%d_%d" % unit, align_bytes=64)
             copy = nc.vector.tensor_copy if on_vector else nc.scalar.copy
             copy(
                 out=o_t[:].bitcast(F32).rearrange("p t (u w) -> p t u w", u=2),
@@ -162,15 +180,18 @@ def tile_token_merging_cosine_scores_d9_kernel(
             kind, i, g = unit
 
             def words(t, u):
-                if unit in perm:
-                    return perm[unit][:, t, PAIR * u : PAIR * (u + 1)].bitcast(F32)
                 if kind == "O":
+                    if unit in perm:
+                        return perm[unit][:, t, PAIR * u : PAIR * (u + 1)].bitcast(F32)
                     return o_sb[i][:, t, PASS * g : PASS * (g + 1)].bitcast(F32)[:, u:PAIR:2]
-                if g == EP:
-                    return p_sb[i][:, t, :].bitcast(F32)[:, u:PAIR:2]
-                if 3 * i + g in CFG["se"]:
-                    return ew[i][g][:, t, :].bitcast(F32)[:, u:PAIR:2]
-                return ew[i][g][:, t, PAIR * u : PAIR * (u + 1)].bitcast(F32)
+                q = FIRST[g][t]
+                if q == EP:
+                    if unit in perm:
+                        return perm[unit][:, 0, PAIR * u : PAIR * (u + 1)].bitcast(F32)
+                    return p_sb[i // 2][:, i % 2, :].bitcast(F32)[:, u:PAIR:2]
+                if (i, q) in CFG["se"] or (i, q) in CFG["vc"]:
+                    return ew[i, q][:].bitcast(F32)[:, u:PAIR:2]
+                return ew[i, q][:, PAIR * u : PAIR * (u + 1)].bitcast(F32)
 
             return turned(words, unit, on_vector)
 
@@ -222,35 +243,33 @@ def tile_token_merging_cosine_scores_d9_kernel(
 
         ro_row = ro[:].rearrange("p n m -> p (n m)")
 
-        def multiply(i, j):
-            acc = accs.tile([NP, 2, PAIR], F32, name="acc")
-            for mt in range(2):
-                for g in range(EP + 1):
-                    cols = slice(128 * mt, 128 * mt + 128)
-                    nc.tensor.matmul_mx(
-                        out=acc[:, mt, :],
-                        lhsT=codes["E", i, g][:, cols].bitcast(FP8X4),
-                        lhsT_scale=scales["E", i, g][:, cols],
-                        rhs=codes["O", j, g][:].bitcast(FP8X4),
-                        rhs_scale=scales["O", j, g][:],
-                        start=(g == 0),
-                        stop=(g == EP),
-                    )
-            return (acc, i, j)
+        def multiply(m, c0, width):
+            acc = accs.tile([NP, 512], F32, name="acc")
+            h, at = divmod(c0, 512)
+            for n, (g, key, c) in enumerate([(EP, 0, 0), (0, 0, 128), (1, 1, 0), (2, 1, 128)]):
+                nc.tensor.matmul_mx(
+                    out=acc[:, :width],
+                    lhsT=codes["E", m, key][:, c : c + 128].bitcast(FP8X4),
+                    lhsT_scale=scales["E", m, key][:, c : c + 128],
+                    rhs=codes["O", h, g][:, at : at + width].bitcast(FP8X4),
+                    rhs_scale=scales["O", h, g][:, at : at + width],
+                    start=(n == 0),
+                    stop=(n == EP),
+                )
+            return (acc, m, c0, width)
 
         def finish(item):
-            acc, i, j = item
-            res = results.tile([NP, 2, PAIR], F32, name="res")
-            for mt in range(2):
-                m = 2 * i + mt
+            acc, m, c0, width = item
+            res = results.tile([NP, 512], F32, name="res")
+            pieces = 2 if len(blocks) == bi and item is made[-1] else 1
+            step = width // pieces
+            for x in range(pieces):
+                a = x * step
                 nc.vector.scalar_tensor_tensor(
-                    out=res[:, mt, :], in0=acc[:, mt, :], scalar=re32[:, m : m + 1],
-                    in1=ro_row[:, PAIR * j : PAIR * (j + 1)], op0=MULT, op1=MULT,
+                    out=res[:, a : a + step], in0=acc[:, a : a + step], scalar=re32[:, m : m + 1],
+                    in1=ro_row[:, c0 + a : c0 + a + step], op0=MULT, op1=MULT,
                 )
-                if (i, j) == (NPAIR - 1, NPAIR - 1):
-                    nc.sync.dma_start(out=out_rows[:, m, PAIR * j : PAIR * (j + 1)], in_=res[:, mt, :])
-            if (i, j) != (NPAIR - 1, NPAIR - 1):
-                nc.sync.dma_start(out=out_rows[:, 2 * i : 2 * i + 2, PAIR * j : PAIR * (j + 1)], in_=res[:])
+                nc.sync.dma_start(out=out_rows[:, m, c0 + a : c0 + a + step], in_=res[:, a : a + step])
 
         warm = keep.tile([NP, 512], BF16, name="warm")
         if any(CFG["dummy"]):
@@ -258,40 +277,44 @@ def tile_token_merging_cosine_scores_d9_kernel(
 
         def dummy(n):
             if n:
-                acc = accs.tile([NP, 2, PAIR], F32, name="acc")
+                acc = accs.tile([NP, 512], F32, name="acc")
                 for x in range(n):
-                    nc.tensor.matmul(acc[:].rearrange("p a n -> p (a n)"), lhsT=warm[:, :NP], rhs=warm[:], start=True, stop=True)
+                    nc.tensor.matmul(acc[:], lhsT=warm[:, :NP], rhs=warm[:], start=True, stop=True)
 
         units = []
-        for s in range(NPAIR):
-            units.extend([("O", s, g) for g in range(EP)])
-            units.extend([("E", s, g) for g in (EP, 0, 1, 2)])
-        chunks = [("E", i, g) for i in range(NPAIR) for g in range(EP)]
-        blocks = []
-        for s in range(NPAIR):
-            blocks.extend([(i, s) for i in range(s)])
-            blocks.extend([(s, j) for j in range(s + 1)])
-
-        def scale_chunk(unit):
-            kind, i, g = unit
-            for mt in range(2):
-                for b in range(4):
-                    if 3 * i + g in CFG["se"]:
-                        src = e8[i][:, mt, PASS * g + 128 * b : PASS * g + 128 * b + 128].bitcast(F8)
-                        nc.scalar.activation(out=ew[i][g][:, mt, 128 * b : 128 * b + 128], in_=src, func=COPY,
-                                             scale=es[:, 2 * i + mt, 4 * g + b : 4 * g + b + 1])
-                    else:
-                        scale_e(i, g, mt, b)
+        for kind, s in CFG["order"]:
+            units.extend([(kind, s, g) for g in ((0, 1, 2) if kind == "O" else (0, 1))])
+        turn_of = {unit: x for x, unit in enumerate(units)}
+        last = {}
+        for x, unit in enumerate(units):
+            last[unit[0], unit[1]] = x
+        todo = []
+        for m in range(8):
+            for h in range(2):
+                ready = max(last["E", m], last["O", 2 * h], last["O", 2 * h + 1])
+                if (m, h) in CFG["split"]:
+                    for j in (2 * h, 2 * h + 1):
+                        todo.append((max(last["E", m], last["O", j]), m, PAIR * j, PAIR))
+                else:
+                    todo.append((ready, m, 512 * h, 512))
+        blocks = sorted([(r + CFG["bd"].get((m, c), CFG["lag"]), r, m, c, w) for r, m, c, w in todo])
+        chunks = []
+        for m in range(8):
+            for g in range(EP):
+                x = turn_of["E", m, 0 if g == 0 else 1]
+                chunks.append((x - CFG["sd"][m], m, g))
+        chunks.sort()
+        gtodo = sorted([(last["O", j] + CFG["gd"][j], j) for j in range(NPAIR)])
 
         dummy(CFG["dummy"][0])
         waiting, made = [], []
         bi = ci = gi = 0
-        for x in range(len(units) + 8):
-            while ci < len(chunks) and CFG["sc"][ci] <= x:
-                scale_chunk(chunks[ci])
+        for x in range(len(units) + 12):
+            while ci < len(chunks) and chunks[ci][0] <= x:
+                scale_e(chunks[ci][1], chunks[ci][2])
                 ci += 1
-            for y in range(x + 1 if x == 0 else x + CFG["pa"], x + CFG["pa"] + 1):
-                if y < len(units) and y in CFG["pp"] and units[y] not in perm:
+            for y in range(1 if x == 0 else x + CFG["pa"], x + CFG["pa"] + 1):
+                if y < len(units) and y in CFG["pp"] and units[y] not in perm and (units[y][0] == "O" or units[y][2] == 0):
                     permute(units[y], CFG["pp"][y])
             if x == CFG["norm"]:
                 norms()
@@ -301,9 +324,10 @@ def tile_token_merging_cosine_scores_d9_kernel(
                 dummy(CFG["dummy"][x + 1])
             if x == CFG["ro"]:
                 spread_o_norm(CFG["rov"])
-            while gi < NPAIR and CFG["g"][gi] <= x:
-                widen_g(gi, CFG["gw"][gi])
-                waiting.append((x + CFG["gl"], group_g(gi, CFG["gg"][gi])))
+            while gi < NPAIR and gtodo[gi][0] <= x:
+                j = gtodo[gi][1]
+                widen_g(j, CFG["gw"][j])
+                waiting.append((x + CFG["gl"], group_g(j, CFG["gg"][j])))
                 gi += 1
             for entry in [e for e in waiting if e[0] <= x]:
                 quantize(entry[1])
@@ -311,16 +335,16 @@ def tile_token_merging_cosine_scores_d9_kernel(
             for d in made:
                 finish(d)
             made = []
-            while bi < len(blocks) and CFG["b"][bi] <= x:
-                i, j = blocks[bi]
+            while bi < len(blocks) and blocks[bi][0] <= x:
+                pos, ready, m, c0, width = blocks[bi]
                 for entry in list(waiting):
                     key = entry[1][1]
-                    if key[:2] == ("E", i) or key[:2] == ("O", j):
+                    if key[:2] == ("E", m) or (key[0] == "O" and PAIR * key[1] < c0 + width and PAIR * key[1] + PAIR > c0):
                         quantize(entry[1])
                         waiting.remove(entry)
                 if len(made) == 3:
                     finish(made.pop(0))
-                made.append(multiply(i, j))
                 bi += 1
+                made.append(multiply(m, c0, width))
         for d in made:
             finish(d)

@@ -20,7 +20,7 @@ PASS = 512
 EP = K // PASS
 PAIR = 256
 NPAIR = T // PAIR
-CFG = {'dummy': [0, 2, 0, 2, 0, 2, 0, 0, 0, 0, 0, 0, 0, 0], 'norm': 1, 'ql': 2, 'cv': [], 'ro': 7, 'rov': False, 'order': [('O', 0), ('E', 0), ('E', 1), ('O', 1), ('E', 2), ('E', 3), ('O', 2), ('E', 4), ('E', 5), ('O', 3), ('E', 6), ('E', 7)], 'sd': [13, 3, 3, 3, 3, 3, 3, 3], 'gd': [-1, -3, -3, -3], 'gw': [True, True, True, True], 'gg': [True, True, False, False], 'gl': 2, 'split': [(0, 0), (1, 0), (2, 0), (0, 1), (1, 1), (2, 1), (3, 1), (4, 1), (5, 1)], 'bd': {}, 'lag': 4, 'se': [(0, 1), (1, 1), (2, 1), (3, 1), (4, 1), (5, 1), (6, 1), (7, 1)], 'vc': [], 'pp': {15: False, 16: False, 22: False, 23: False, 24: False, 26: False}, 'pa': 4, 'head': ['o0', 'e0', 'o1', 'o2', 'g', 'p', 'e1'], 'ord': 'b', 'sd1': 4, 'gd0': 0, 'gwv': 0, 'ggv': 4, 'sp0': 1, 'sp1': 2, 'sem': 4, 'seg': (0,), 'po': 3, 'pog': (1,), 'pm': 8, 'pv': False, 'cvs': 28, 'cvn': 9, 'cve': 14, 'd0': 3, 'd1': 8, 'dn': 2, 'dc': 2}
+CFG = {'dummy': [0, 0, 0, 2, 0, 2, 0, 2, 0, 0, 0, 0, 0, 0], 'norm': 5, 'ql': 2, 'cv': [5], 'ro': 7, 'rov': False, 'order': [('O', 0), ('E', 0), ('O', 1), ('E', 1), ('E', 2), ('E', 3), ('O', 2), ('O', 3), ('E', 4), ('E', 5), ('E', 6), ('E', 7)], 'sd': [13, 4, 3, 3, 3, 3, 3, 3], 'gd': [2, -1, -1, -1], 'gw': [True, True, True, True], 'gg': [False, False, False, False], 'gl': 2, 'split': [(0, 0), (1, 0), (2, 0), (3, 0), (4, 0), (5, 0), (6, 0), (7, 0), (0, 1), (1, 1), (2, 1), (3, 1), (4, 1), (5, 1), (6, 1), (7, 1)], 'bd': {}, 'lag': 4, 'se': [(4, 1), (5, 1), (6, 1), (7, 1)], 'vc': [], 'pp': {16: False, 19: False, 20: False, 22: False, 24: False, 26: False}, 'pa': 6, 'head': ['o0', 'e0', 'o1', 'o2', 'g', 'p', 'e1'], 'ord': 'c', 'sd1': 4, 'gd0': 2, 'gwv': 3, 'ggv': 1, 'sp0': 8, 'sp1': 8, 'sem': 1, 'seg': (1,), 'po': 3, 'pog': (1, 2), 'pm': 4, 'pv': False, 'cvs': 28, 'cvn': 2, 'cve': 28, 'd0': 1, 'd1': 6, 'dn': 2, 'dc': 2}
 
 
 def tile_token_merging_cosine_scores_d9_kernel(
@@ -54,8 +54,8 @@ def tile_token_merging_cosine_scores_d9_kernel(
             e8.append(e_t)
             p_t = keep.tile([NP, 2, R], BF16, name=f"p_sb{j}", align_bytes=64)
             p_sb.append(p_t)
-        for h in range(NPAIR):
-            g_t = keep.tile([NP, 4, PAIR], U8, name=f"g8_{h}", align_bytes=64)
+        for h in range(2):
+            g_t = keep.tile([NP, 4, 512], U8, name=f"g8_{h}", align_bytes=64)
             g8.append(g_t)
 
         def load_o(j, cols):
@@ -71,34 +71,41 @@ def tile_token_merging_cosine_scores_d9_kernel(
             nc.sync.dma_start(out=p_sb[i][:], in_=p_rows[:, 2 * i : 2 * i + 2, :])
 
         def load_g(h):
-            nc.sync.dma_start(out=g8[h][:], in_=g_rows[:, :, PAIR * h : PAIR * (h + 1)])
+            nc.sync.dma_start(out=g8[h][:], in_=g_rows[:, :, 512 * h : 512 * (h + 1)])
 
         def load_e_tile(m, cols=slice(0, K)):
             nc.sync.dma_start(out=e8[m // 2][:, m % 2, cols], in_=e_rows[:, m, cols])
 
         for what in CFG["head"]:
-            if what[0] == "o":
+            if what == "oR":
+                load_o(0, slice(PASS, K))
+            elif what[0] == "o":
                 load_o(0, slice(PASS * int(what[1]), PASS * int(what[1]) + PASS))
+            elif what == "E":
+                load_e(0)
             elif what[0] == "e":
                 load_e_tile(int(what[1]))
             elif what[0] == "p":
                 load_p(0)
             else:
                 load_g(0)
-        nc.scalar.dma_start(out=on[:], in_=o_norm.rearrange("(p m) -> p m", m=8))
-        nc.scalar.dma_start(out=en[:], in_=e_norm.rearrange("(p m) -> p m", m=8))
+        ident = keep.tile([NP, NP], F32, name="ident")
+        make_identity(nc, ident[:])
+        gall = keep.tile([NP, 4, 8], F32, name="gall")
+        nc.gpsimd.dma_start(out=gall[:].rearrange("p a b -> p (a b)"), in_=G_scale.rearrange("a b -> (a b)").partition_broadcast(NP))
+        nc.gpsimd.dma_start(out=on[:], in_=o_norm.rearrange("(p m) -> p m", m=8))
+        nc.gpsimd.dma_start(out=en[:], in_=e_norm.rearrange("(p m) -> p m", m=8))
         for a in range(4):
-            nc.scalar.dma_start(out=gs[32 * a : 32 * a + 32, :], in_=G_scale[a].partition_broadcast(32))
+            rows = slice(32 * a, 32 * a + 32)
+            nc.gpsimd.tensor_copy(out=gs[rows, :], in_=gall[rows, a, :])
         for kind, j in CFG["order"]:
             if kind == "O" and j > 0:
                 load_o(j, slice(0, K))
-                load_g(j)
+                if j == 2:
+                    load_g(1)
             elif kind == "E" and j % 2 == 0 and j > 0:
                 load_e(j // 2)
                 load_p(j // 2)
-
-        ident = keep.tile([NP, NP], F32, name="ident")
-        make_identity(nc, ident[:])
 
         ew = {}
         for m in range(8):
@@ -106,8 +113,8 @@ def tile_token_merging_cosine_scores_d9_kernel(
                 w_t = keep.tile([NP, PASS], BF16, name=f"ew{m}_{g}", align_bytes=64)
                 ew[m, g] = w_t
         gw = []
-        for h in range(NPAIR):
-            w_t = keep.tile([NP, 4, PAIR], BF16, name=f"gw{h}", align_bytes=64)
+        for h in range(2):
+            w_t = keep.tile([NP, 4, 512], BF16, name=f"gw{h}", align_bytes=64)
             gw.append(w_t)
 
         codes, scales = {}, {}
@@ -206,9 +213,9 @@ def tile_token_merging_cosine_scores_d9_kernel(
         def group_g(j, on_vector):
             grouped = stage.tile([NP, 4 * PAIR], BF16, name="grouped", align_bytes=64)
             dst = grouped[:].rearrange("p (c t) -> p c t", t=4)
-            src = gw[j][:].rearrange("p t n -> p n t")
+            src = gw[j // 2][:].rearrange("p t n -> p n t")
             for b in range(2):
-                c0 = 128 * b
+                c0 = PAIR * (j % 2) + 128 * b
                 col = gs[:, 2 * j + b : 2 * j + b + 1]
                 if on_vector:
                     nc.vector.tensor_scalar(
@@ -273,7 +280,7 @@ def tile_token_merging_cosine_scores_d9_kernel(
 
         warm = keep.tile([NP, 512], BF16, name="warm")
         if any(CFG["dummy"]):
-            nc.gpsimd.memset(warm[:], 1.0)
+            nc.vector.memset(warm[:], 1.0)
 
         def dummy(n):
             if n:
@@ -326,7 +333,8 @@ def tile_token_merging_cosine_scores_d9_kernel(
                 spread_o_norm(CFG["rov"])
             while gi < NPAIR and gtodo[gi][0] <= x:
                 j = gtodo[gi][1]
-                widen_g(j, CFG["gw"][j])
+                if j % 2 == 0:
+                    widen_g(j // 2, CFG["gw"][j])
                 waiting.append((x + CFG["gl"], group_g(j, CFG["gg"][j])))
                 gi += 1
             for entry in [e for e in waiting if e[0] <= x]:

@@ -20,7 +20,7 @@ PASS = 512
 EP = K // PASS
 PAIR = 256
 NPAIR = T // PAIR
-CFG = {'dummy': [0, 0, 0, 2, 0, 2, 0, 2, 0, 0, 0, 0, 0, 0], 'norm': 5, 'ql': 2, 'cv': [5], 'ro': 7, 'rov': False, 'order': [('O', 0), ('E', 0), ('O', 1), ('E', 1), ('E', 2), ('E', 3), ('O', 2), ('O', 3), ('E', 4), ('E', 5), ('E', 6), ('E', 7)], 'sd': [13, 4, 3, 3, 3, 3, 3, 3], 'gd': [2, -1, -1, -1], 'gw': [True, True, True, True], 'gg': [False, False, False, False], 'gl': 2, 'split': [(0, 0), (1, 0), (2, 0), (3, 0), (4, 0), (5, 0), (6, 0), (7, 0), (0, 1), (1, 1), (2, 1), (3, 1), (4, 1), (5, 1), (6, 1), (7, 1)], 'bd': {}, 'lag': 4, 'se': [(4, 1), (5, 1), (6, 1), (7, 1)], 'vc': [], 'pp': {16: False, 19: False, 20: False, 22: False, 24: False, 26: False}, 'pa': 6, 'head': ['o0', 'e0', 'o1', 'o2', 'g', 'p', 'e1'], 'ord': 'c', 'sd1': 4, 'gd0': 2, 'gwv': 3, 'ggv': 1, 'sp0': 8, 'sp1': 8, 'sem': 1, 'seg': (1,), 'po': 3, 'pog': (1, 2), 'pm': 4, 'pv': False, 'cvs': 28, 'cvn': 2, 'cve': 28, 'd0': 1, 'd1': 6, 'dn': 2, 'dc': 2}
+CFG = {'dummy': [0, 2, 0, 2, 0, 2, 0, 2, 0, 0, 0, 0, 0, 0], 'norm': 4, 'ql': 2, 'cv': [], 'ro': 7, 'rov': False, 'order': [('E', 0), ('O', 0), ('E', 1), ('O', 1), ('E', 2), ('E', 3), ('O', 2), ('E', 4), ('E', 5), ('O', 3), ('E', 6), ('E', 7)], 'sd': [13, 6, 4, 4, 4, 4, 4, 4], 'gd': [0, -3, -3, -3], 'gw': [True, True, True, True], 'gg': [True, False, False, False], 'gl': 2, 'split': [(0, 0), (1, 0), (0, 1), (1, 1)], 'bd': {}, 'lag': 4, 'se': [], 'vc': [], 'pp': {15: False, 17: False, 19: False, 22: False, 24: False, 26: False}, 'pa': 4, 'head': ['e0', 'p', 'e1', 'o0', 'o1', 'o2', 'g'], 'ord': 'h', 'sd1': 6, 'gd0': 0, 'gwv': 4, 'ggv': 1, 'sp0': 2, 'sp1': 2, 'sem': 2, 'seg': (), 'po': 2, 'pog': (1,), 'pm': 4, 'pv': False, 'cvs': 28, 'cvn': 4, 'cve': 8, 'd0': 1, 'd1': 8, 'dn': 2, 'dc': 2, 'grp': 2, 'gph': 0}
 
 
 def tile_token_merging_cosine_scores_d9_kernel(
@@ -45,6 +45,8 @@ def tile_token_merging_cosine_scores_d9_kernel(
         en = keep.tile([NP, 8], BF16, name="en")
         on = keep.tile([NP, 8], BF16, name="on")
         gs = keep.tile([NP, 8], F32, name="gs")
+        for a in range(4):
+            nc.scalar.dma_start(out=gs[32 * a : 32 * a + 32, :], in_=G_scale[a].partition_broadcast(32))
 
         o_sb, e8, p_sb, g8 = [], [], [], []
         for j in range(NPAIR):
@@ -91,13 +93,8 @@ def tile_token_merging_cosine_scores_d9_kernel(
                 load_g(0)
         ident = keep.tile([NP, NP], F32, name="ident")
         make_identity(nc, ident[:])
-        gall = keep.tile([NP, 4, 8], F32, name="gall")
-        nc.gpsimd.dma_start(out=gall[:].rearrange("p a b -> p (a b)"), in_=G_scale.rearrange("a b -> (a b)").partition_broadcast(NP))
-        nc.gpsimd.dma_start(out=on[:], in_=o_norm.rearrange("(p m) -> p m", m=8))
-        nc.gpsimd.dma_start(out=en[:], in_=e_norm.rearrange("(p m) -> p m", m=8))
-        for a in range(4):
-            rows = slice(32 * a, 32 * a + 32)
-            nc.gpsimd.tensor_copy(out=gs[rows, :], in_=gall[rows, a, :])
+        nc.sync.dma_start(out=on[:], in_=o_norm.rearrange("(p m) -> p m", m=8))
+        nc.sync.dma_start(out=en[:], in_=e_norm.rearrange("(p m) -> p m", m=8))
         for kind, j in CFG["order"]:
             if kind == "O" and j > 0:
                 load_o(j, slice(0, K))
@@ -343,7 +340,7 @@ def tile_token_merging_cosine_scores_d9_kernel(
             for d in made:
                 finish(d)
             made = []
-            while bi < len(blocks) and blocks[bi][0] <= x:
+            while bi < len(blocks) and blocks[bi][0] <= x and (x % CFG["grp"] == CFG["gph"] or x >= len(units)):
                 pos, ready, m, c0, width = blocks[bi]
                 for entry in list(waiting):
                     key = entry[1][1]

from contextlib import ExitStack

import concourse.mybir as mybir
from concourse.masks import make_identity

T, U, K, R = 1024, 1024, 1536, 512
FLOPS = 2 * T * U * (K + R)

F32 = mybir.dt.float32
BF16 = mybir.dt.bfloat16
U32 = mybir.dt.uint32
U8 = mybir.dt.uint8
F8 = mybir.dt.float8_e4m3fn
FP8X4 = mybir.dt.float8_e4m3fn_x4
MULT = mybir.AluOpType.mult
COPY = mybir.ActivationFunctionType.Copy

NP = 128
PASS = 512
EP = K // PASS
PAIR = 256
NPAIR = T // PAIR
CFG = {'dummy': [0, 2, 0, 2, 0, 2, 0, 2, 0, 0, 0, 0, 0, 0], 'norm': 4, 'ql': 2, 'cv': [], 'ro': 7, 'rov': False, 'order': [('E', 0), ('O', 0), ('E', 1), ('O', 1), ('E', 2), ('E', 3), ('O', 2), ('E', 4), ('E', 5), ('O', 3), ('E', 6), ('E', 7)], 'sd': [13, 6, 4, 4, 4, 4, 4, 4], 'gd': [0, -3, -3, -3], 'gw': [True, True, True, True], 'gg': [True, False, False, False], 'gl': 2, 'split': [(0, 0), (1, 0), (0, 1), (1, 1)], 'bd': {}, 'lag': 4, 'se': [], 'vc': [], 'pp': {15: False, 17: False, 19: False, 22: False, 24: False, 26: False}, 'pa': 4, 'head': ['e0', 'p', 'e1', 'o0', 'o1', 'o2', 'g'], 'ord': 'h', 'sd1': 6, 'gd0': 0, 'gwv': 4, 'ggv': 1, 'sp0': 2, 'sp1': 2, 'sem': 2, 'seg': (), 'po': 2, 'pog': (1,), 'pm': 4, 'pv': False, 'cvs': 28, 'cvn': 4, 'cve': 8, 'd0': 1, 'd1': 8, 'dn': 2, 'dc': 2, 'grp': 2, 'gph': 0}


def tile_token_merging_cosine_scores_d9_kernel(
    tc, E_bytes, E_scale, O, P, G_bytes, G_scale, e_norm, o_norm, out
):
    nc = tc.nc
    with ExitStack() as ctx:
        keep = ctx.enter_context(tc.tile_pool(name="keep", bufs=1))
        stage = ctx.enter_context(tc.tile_pool(name="stage", bufs=8))
        results = ctx.enter_context(tc.tile_pool(name="results", bufs=8))
        turn = ctx.enter_context(tc.psum_pool(name="turn", bufs=4))
        accs = ctx.enter_context(tc.psum_pool(name="accs", bufs=4))
        ctx.enter_context(tc.manual_schedule())

        e_rows = E_bytes.rearrange("(p m) k -> p m k", m=8)
        p_rows = P.rearrange("(p m) k -> p m k", m=8)
        out_rows = out.rearrange("(p m) n -> p m n", m=8)
        g_rows = G_bytes.rearrange("(p t) n -> p t n", t=4)

        es = keep.tile([NP, 8, 12], F32, name="es")
        nc.scalar.dma_start(out=es[:], in_=E_scale.rearrange("(p m) b -> p m b", m=8))
        en = keep.tile([NP, 8], BF16, name="en")
        on = keep.tile([NP, 8], BF16, name="on")
        gs = keep.tile([NP, 8], F32, name="gs")
        for a in range(4):
            nc.scalar.dma_start(out=gs[32 * a : 32 * a + 32, :], in_=G_scale[a].partition_broadcast(32))

        o_sb, e8, p_sb, g8 = [], [], [], []
        for j in range(NPAIR):
            o_t = keep.tile([NP, 2, K], BF16, name=f"o_sb{j}", align_bytes=64)
            o_sb.append(o_t)
            e_t = keep.tile([NP, 2, K], U8, name=f"e8_{j}", align_bytes=64)
            e8.append(e_t)
            p_t = keep.tile([NP, 2, R], BF16, name=f"p_sb{j}", align_bytes=64)
            p_sb.append(p_t)
        for h in range(2):
            g_t = keep.tile([NP, 4, 512], U8, name=f"g8_{h}", align_bytes=64)
            g8.append(g_t)

        def load_o(j, cols):
            nc.sync.dma_start(
                out=o_sb[j][:, :, cols],
                in_=O[PAIR * j : PAIR * (j + 1), cols].rearrange("(t p) k -> p t k", p=NP),
            )

        def load_e(i, cols=slice(0, K)):
            nc.sync.dma_start(out=e8[i][:, :, cols], in_=e_rows[:, 2 * i : 2 * i + 2, cols])

        def load_p(i):
            nc.sync.dma_start(out=p_sb[i][:], in_=p_rows[:, 2 * i : 2 * i + 2, :])

        def load_g(h):
            nc.sync.dma_start(out=g8[h][:], in_=g_rows[:, :, 512 * h : 512 * (h + 1)])

        def load_e_tile(m, cols=slice(0, K)):
            nc.sync.dma_start(out=e8[m // 2][:, m % 2, cols], in_=e_rows[:, m, cols])

        for what in CFG["head"]:
            if what == "oR":
                load_o(0, slice(PASS, K))
            elif what[0] == "o":
                load_o(0, slice(PASS * int(what[1]), PASS * int(what[1]) + PASS))
            elif what == "E":
                load_e(0)
            elif what[0] == "e":
                load_e_tile(int(what[1]))
            elif what[0] == "p":
                load_p(0)
            else:
                load_g(0)
        ident = keep.tile([NP, NP], F32, name="ident")
        make_identity(nc, ident[:])
        nc.sync.dma_start(out=on[:], in_=o_norm.rearrange("(p m) -> p m", m=8))
        nc.sync.dma_start(out=en[:], in_=e_norm.rearrange("(p m) -> p m", m=8))
        for kind, j in CFG["order"]:
            if kind == "O" and j > 0:
                load_o(j, slice(0, K))
                if j == 2:
                    load_g(1)
            elif kind == "E" and j % 2 == 0 and j > 0:
                load_e(j // 2)
                load_p(j // 2)

        ew = {}
        for m in range(8):
            for g in range(EP):
                w_t = keep.tile([NP, PASS], BF16, name=f"ew{m}_{g}", align_bytes=64)
                ew[m, g] = w_t
        gw = []
        for h in range(2):
            w_t = keep.tile([NP, 4, 512], BF16, name=f"gw{h}", align_bytes=64)
            gw.append(w_t)

        codes, scales = {}, {}

        def scale_e(m, g):
            for b in range(4):
                c0 = PASS * g + 128 * b
                src = e8[m // 2][:, m % 2, c0 : c0 + 128].bitcast(F8)
                col = es[:, m, 4 * g + b : 4 * g + b + 1]
                if (m, g) in CFG["se"]:
                    nc.scalar.activation(out=ew[m, g][:, 128 * b : 128 * b + 128], in_=src, func=COPY, scale=col)
                elif (m, g) in CFG["vc"]:
                    nc.vector.tensor_scalar(out=ew[m, g][:, 128 * b : 128 * b + 128], in0=src, scalar1=col, scalar2=None, op0=MULT)
                else:
                    dst = ew[m, g][:].rearrange("q (u p e) -> q p u e", u=2, e=2)[:, 32 * b : 32 * b + 32]
                    nc.vector.tensor_scalar(out=dst, in0=src.rearrange("q (p u e) -> q p u e", u=2, e=2),
                                            scalar1=col, scalar2=None, op0=MULT)

        def turned(source, key, on_vector):
            bank = turn.tile([NP, 2, 2, NP], F32, name="bank")
            for t in range(2):
                for u in range(2):
                    nc.tensor.transpose(bank[:, t, u, :], source(t, u), ident[:])
            grouped = stage.tile([NP, 4 * PAIR], BF16, name="grouped", align_bytes=64)
            copy = nc.vector.tensor_copy if on_vector else nc.scalar.copy
            copy(
                out=grouped[:].bitcast(F32).rearrange("p (t r u) -> p t r u", t=2, u=2),
                in_=bank[:].rearrange("p t u r -> p t r u"),
            )
            return (grouped, key)

        def quantize(item):
            grouped, key = item
            kind, i, g = key
            if kind == "O":
                home, at = ("O", i // 2, g), PAIR * (i % 2)
                if home not in codes:
                    c_t = keep.tile([NP, 2 * PAIR], U32, name="codes_%s_%d_%d" % home, align_bytes=64)
                    s_t = keep.tile([NP, 2 * PAIR], U8, name="scales_%s_%d_%d" % home, align_bytes=64)
                    codes[home], scales[home] = c_t, s_t
            else:
                home, at = key, 0
                c_t = keep.tile([NP, PAIR], U32, name="codes_%s_%d_%d" % home, align_bytes=64)
                s_t = keep.tile([NP, PAIR], U8, name="scales_%s_%d_%d" % home, align_bytes=64)
                codes[home], scales[home] = c_t, s_t
            nc.vector.quantize_mx(
                out=codes[home][:, at : at + PAIR].bitcast(FP8X4),
                scales=scales[home][:, at : at + PAIR],
                in_=grouped[:],
            )

        perm = {}
        FIRST = {0: (EP, 0), 1: (1, 2)}

        def permute(unit, on_vector):
            kind, i, g = unit
            if kind == "O":
                src, n = o_sb[i][:, :, PASS * g : PASS * (g + 1)], 2
            else:
                src, n = p_sb[i // 2][:, i % 2 : i % 2 + 1, :], 1
            o_t = keep.tile([NP, n, PASS], BF16, name="perm_%s_%d_%d" % unit, align_bytes=64)
            copy = nc.vector.tensor_copy if on_vector else nc.scalar.copy
            copy(
                out=o_t[:].bitcast(F32).rearrange("p t (u w) -> p t u w", u=2),
                in_=src.bitcast(F32).rearrange("p t (w u) -> p t u w", u=2),
            )
            perm[unit] = o_t

        def turn_bank(unit, on_vector):
            kind, i, g = unit

            def words(t, u):
                if kind == "O":
                    if unit in perm:
                        return perm[unit][:, t, PAIR * u : PAIR * (u + 1)].bitcast(F32)
                    return o_sb[i][:, t, PASS * g : PASS * (g + 1)].bitcast(F32)[:, u:PAIR:2]
                q = FIRST[g][t]
                if q == EP:
                    if unit in perm:
                        return perm[unit][:, 0, PAIR * u : PAIR * (u + 1)].bitcast(F32)
                    return p_sb[i // 2][:, i % 2, :].bitcast(F32)[:, u:PAIR:2]
                if (i, q) in CFG["se"] or (i, q) in CFG["vc"]:
                    return ew[i, q][:].bitcast(F32)[:, u:PAIR:2]
                return ew[i, q][:, PAIR * u : PAIR * (u + 1)].bitcast(F32)

            return turned(words, unit, on_vector)

        def widen_g(h, on_vector):
            src = g8[h][:].rearrange("p t n -> p (t n)").bitcast(F8)
            dst = gw[h][:].rearrange("p t n -> p (t n)")
            if on_vector:
                nc.vector.tensor_copy(out=dst, in_=src)
            else:
                nc.scalar.copy(out=dst, in_=src)

        def group_g(j, on_vector):
            grouped = stage.tile([NP, 4 * PAIR], BF16, name="grouped", align_bytes=64)
            dst = grouped[:].rearrange("p (c t) -> p c t", t=4)
            src = gw[j // 2][:].rearrange("p t n -> p n t")
            for b in range(2):
                c0 = PAIR * (j % 2) + 128 * b
                col = gs[:, 2 * j + b : 2 * j + b + 1]
                if on_vector:
                    nc.vector.tensor_scalar(
                        out=dst[:, 128 * b : 128 * b + 128, :], in0=src[:, c0 : c0 + 128, :],
                        scalar1=col, scalar2=None, op0=MULT,
                    )
                else:
                    nc.scalar.activation(
                        out=dst[:, 128 * b : 128 * b + 128, :], in_=src[:, c0 : c0 + 128, :],
                        func=COPY, scale=col,
                    )
            return (grouped, ("O", j, EP))

        re32 = keep.tile([NP, 8], F32, name="re32")
        re = keep.tile([NP, 8], F32, name="re")
        r8 = keep.tile([NP, 8], F32, name="r8")
        ro = keep.tile([NP, NP, 8], F32, name="ro")

        def norms():
            nc.vector.reciprocal(out=r8[:], in_=on[:])
            nc.vector.reciprocal(out=re[:], in_=en[:])
            nc.vector.tensor_scalar(out=re32[:], in0=re[:], scalar1=32.0, scalar2=None, op0=MULT)

        def spread_o_norm(on_vector):
            for h in range(2):
                bank = turn.tile([NP, 4, NP], F32, name="bank")
                for q in range(4):
                    m = 4 * h + q
                    nc.tensor.transpose(bank[:, q, :], r8[:, m : m + 1].to_broadcast([NP, NP]), ident[:])
                copy = nc.vector.tensor_copy if on_vector else nc.scalar.copy
                copy(out=ro[:, :, 4 * h : 4 * h + 4], in_=bank[:].rearrange("p q n -> p n q"))

        ro_row = ro[:].rearrange("p n m -> p (n m)")

        def multiply(m, c0, width):
            acc = accs.tile([NP, 512], F32, name="acc")
            h, at = divmod(c0, 512)
            for n, (g, key, c) in enumerate([(EP, 0, 0), (0, 0, 128), (1, 1, 0), (2, 1, 128)]):
                nc.tensor.matmul_mx(
                    out=acc[:, :width],
                    lhsT=codes["E", m, key][:, c : c + 128].bitcast(FP8X4),
                    lhsT_scale=scales["E", m, key][:, c : c + 128],
                    rhs=codes["O", h, g][:, at : at + width].bitcast(FP8X4),
                    rhs_scale=scales["O", h, g][:, at : at + width],
                    start=(n == 0),
                    stop=(n == EP),
                )
            return (acc, m, c0, width)

        def finish(item):
            acc, m, c0, width = item
            res = results.tile([NP, 512], F32, name="res")
            pieces = 2 if len(blocks) == bi and item is made[-1] else 1
            step = width // pieces
            for x in range(pieces):
                a = x * step
                nc.vector.scalar_tensor_tensor(
                    out=res[:, a : a + step], in0=acc[:, a : a + step], scalar=re32[:, m : m + 1],
                    in1=ro_row[:, c0 + a : c0 + a + step], op0=MULT, op1=MULT,
                )
                nc.sync.dma_start(out=out_rows[:, m, c0 + a : c0 + a + step], in_=res[:, a : a + step])

        warm = keep.tile([NP, 512], BF16, name="warm")
        if any(CFG["dummy"]):
            nc.vector.memset(warm[:], 1.0)

        def dummy(n):
            if n:
                acc = accs.tile([NP, 512], F32, name="acc")
                for x in range(n):
                    nc.tensor.matmul(acc[:], lhsT=warm[:, :NP], rhs=warm[:], start=True, stop=True)

        units = []
        for kind, s in CFG["order"]:
            units.extend([(kind, s, g) for g in ((0, 1, 2) if kind == "O" else (0, 1))])
        turn_of = {unit: x for x, unit in enumerate(units)}
        last = {}
        for x, unit in enumerate(units):
            last[unit[0], unit[1]] = x
        todo = []
        for m in range(8):
            for h in range(2):
                ready = max(last["E", m], last["O", 2 * h], last["O", 2 * h + 1])
                if (m, h) in CFG["split"]:
                    for j in (2 * h, 2 * h + 1):
                        todo.append((max(last["E", m], last["O", j]), m, PAIR * j, PAIR))
                else:
                    todo.append((ready, m, 512 * h, 512))
        blocks = sorted([(r + CFG["bd"].get((m, c), CFG["lag"]), r, m, c, w) for r, m, c, w in todo])
        chunks = []
        for m in range(8):
            for g in range(EP):
                x = turn_of["E", m, 0 if g == 0 else 1]
                chunks.append((x - CFG["sd"][m], m, g))
        chunks.sort()
        gtodo = sorted([(last["O", j] + CFG["gd"][j], j) for j in range(NPAIR)])

        dummy(CFG["dummy"][0])
        waiting, made = [], []
        bi = ci = gi = 0
        for x in range(len(units) + 12):
            while ci < len(chunks) and chunks[ci][0] <= x:
                scale_e(chunks[ci][1], chunks[ci][2])
                ci += 1
            for y in range(1 if x == 0 else x + CFG["pa"], x + CFG["pa"] + 1):
                if y < len(units) and y in CFG["pp"] and units[y] not in perm and (units[y][0] == "O" or units[y][2] == 0):
                    permute(units[y], CFG["pp"][y])
            if x == CFG["norm"]:
                norms()
            if x < len(units):
                waiting.append((x + CFG["ql"], turn_bank(units[x], x in CFG["cv"])))
            if x + 1 < len(CFG["dummy"]):
                dummy(CFG["dummy"][x + 1])
            if x == CFG["ro"]:
                spread_o_norm(CFG["rov"])
            while gi < NPAIR and gtodo[gi][0] <= x:
                j = gtodo[gi][1]
                if j % 2 == 0:
                    widen_g(j // 2, CFG["gw"][j])
                waiting.append((x + CFG["gl"], group_g(j, CFG["gg"][j])))
                gi += 1
            for entry in [e for e in waiting if e[0] <= x]:
                quantize(entry[1])
                waiting.remove(entry)
            for d in made:
                finish(d)
            made = []
            while bi < len(blocks) and blocks[bi][0] <= x and (x % CFG["grp"] == CFG["gph"] or x >= len(units)):
                pos, ready, m, c0, width = blocks[bi]
                for entry in list(waiting):
                    key = entry[1][1]
                    if key[:2] == ("E", m) or (key[0] == "O" and PAIR * key[1] < c0 + width and PAIR * key[1] + PAIR > c0):
                        quantize(entry[1])
                        waiting.remove(entry)
                if len(made) == 3:
                    finish(made.pop(0))
                bi += 1
                made.append(multiply(m, c0, width))
        for d in made:
            finish(d)
